import numpy as np
import ml_dtypes


def mxq(x, axis, fmt="e4m3"):
    dtype, down = {"e4m3": (ml_dtypes.float8_e4m3fn, 7), "e5m2": (ml_dtypes.float8_e5m2, 14)}[fmt]
    v = np.moveaxis(np.asarray(x, np.float32).astype(ml_dtypes.bfloat16).astype(np.float64), axis, -1)
    blocks = v.reshape(v.shape[:-1] + (-1, 32))
    amax = np.abs(blocks).max(-1, keepdims=True)
    byte = np.maximum(np.where(amax > 0, np.frexp(amax)[1] - 1 + 127, 0) - down, 1)
    scale = np.exp2(byte - 127.0)
    codes = (blocks / scale).astype(np.float32).astype(dtype).astype(np.float64)
    return np.moveaxis((codes * scale).reshape(v.shape), -1, axis)


WIDE = False


def mx_kscale(k):
    if not WIDE:
        return np.ones(k)
    levels = np.array([10, -10, 5, -5, 0])
    if k % 512:
        return np.exp2(np.random.permutation(np.resize(levels, k // 32))).repeat(32)
    a = np.empty((k // 512, 16))
    for p in range(k // 512):
        a[p, :8] = np.random.permutation(np.resize(levels, 8))
        for g in range(8):
            far = levels[np.abs(levels - a[p, g]) >= 10]
            a[p, g + 8] = far[np.random.randint(len(far))]
    return np.exp2(a.ravel()).repeat(32)


def f64(x):
    return np.asarray(x).astype(np.float64)


def striped(idx):
    return np.tile(idx.reshape(-1, 16).T, (8, 1)).astype(np.uint16)


def unstriped(offs):
    return offs[:16].T.reshape(-1).astype(np.int64)


E2M1 = np.array([0.0, 0.5, 1.0, 1.5, 2.0, 3.0, 4.0, 6.0, -0.0, -0.5, -1.0, -1.5, -2.0, -3.0, -4.0, -6.0])


def pack_weight(w, fmt):
    k, n = w.shape
    w = f64(np.asarray(w, np.float32).astype(ml_dtypes.bfloat16)).reshape(k // 32, 32, n)
    amax = np.abs(w).max(1)
    if fmt == "e4m3":
        byte = np.frexp(amax)[1] - 1 + 127 - 7
    else:
        mant, ex = np.frexp(amax / 6.0)
        byte = np.where(mant > 0.5, ex, ex - 1) + 127
    byte = np.clip(np.where(amax > 0, byte, 1), 1, 254)
    scaled = (w * np.exp2(127.0 - byte)[:, None, :]).reshape(k, n).astype(np.float32)
    by_word = np.ascontiguousarray(scaled.reshape(k // 512, 128, 4, n).transpose(0, 1, 3, 2))
    if fmt == "e4m3":
        words = by_word.astype(ml_dtypes.float8_e4m3fn).view(np.uint8)
    else:
        c = by_word.astype(ml_dtypes.float4_e2m1fn).view(np.uint8) & 0xF
        words = (c[..., 0::2] | (c[..., 1::2] << 4)).reshape(k // 512, 128, 2 * n)
    return np.ascontiguousarray(words), np.ascontiguousarray(byte.astype(np.uint8).reshape(k // 512, 16, n))


def unpack_weight(words, scales, fmt):
    g, _, n = scales.shape
    words = np.ascontiguousarray(words).reshape(g, 128, n, -1)
    if fmt == "e4m3":
        vals = words.view(ml_dtypes.float8_e4m3fn).astype(np.float64)
    else:
        nib = np.empty((g, 128, n, 4), np.uint8)
        nib[..., 0::2] = words & 0xF
        nib[..., 1::2] = words >> 4
        vals = E2M1[nib]
    vals = vals * np.repeat(np.exp2(scales.astype(np.float64) - 127.0), 8, axis=1)[..., None]
    return vals.transpose(0, 1, 3, 2).reshape(g * 512, n)


def gelu(v):
    return 0.5 * v * (1.0 + np.tanh(np.sqrt(2.0 / np.pi) * (v + 0.044715 * v**3)))


T, S, P, K, H, N = 4096, 1024, 512, 1536, 1024, 384


def setup_inputs():
    n = np.random.standard_normal
    s = mx_kscale(K)[:, None]
    u = mx_kscale(H)[:, None]
    tab_words, tab_scales = pack_weight(n((K, T)) * s, "e4m3")
    w4_words, w4_scales = pack_weight(n((H, N)) * 0.5 / np.sqrt(H) / u, "e2m1")
    perm = np.random.permutation(S)
    return {
        "tab_words": tab_words,
        "tab_scales": tab_scales,
        "offs": striped(np.random.permutation(T)[:S]),
        "pos1": striped(perm[:P]),
        "pos2": striped(perm[P:]),
        "w1": (n((K, H)) * 0.85 / np.sqrt(K) / s).astype(np.float32),
        "slope": np.random.uniform(0.6, 3.0, H).astype(np.float32),
        "thr": n(H).astype(np.float32),
        "paint": (1.4 * n((H, P))).astype(np.float32),
        "skip": np.random.uniform(0.4, 1.6, H).astype(np.float32),
        "wgs": np.exp(0.3 * n((128, P))).astype(np.float32),
        "gain": (np.random.uniform(0.5, 1.5, H) * u[:, 0]).astype(np.float32),
        "w4_words": w4_words,
        "w4_scales": w4_scales,
        "w5": (n((H, N)) * 0.55 / np.sqrt(H) / u).astype(np.float32),
    }


def reference(tab_words, tab_scales, offs, pos1, pos2, w1, slope, thr, paint,
              skip, wgs, gain, w4_words, w4_scales, w5):
    v = unpack_weight(tab_words, tab_scales, "e4m3")[:, unstriped(offs)]
    w4 = unpack_weight(w4_words, w4_scales, "e2m1")
    h = mxq(f64(w1), 0, "e4m3").T @ v
    look = 1.0 / (1.0 + np.exp(-(f64(slope)[:, None] * h[:, unstriped(pos1)] + f64(thr)[:, None])))
    a = f64(paint) * look
    page = f64(skip)[:, None] * h
    page[:, unstriped(pos2)] = np.tile(f64(wgs), (H // 128, 1)) * a
    pq = mxq(f64(gain)[:, None] * page, 0, "e4m3")
    flat = w4.T @ pq
    wavy = mxq(f64(w5), 0, "e4m3").T @ pq
    return flat + np.sin(wavy)

@@ -1,0 +1,318 @@
+from contextlib import ExitStack
+
+import concourse.mybir as mybir
+
+T, S, PICK, K, H, N = 4096, 1024, 512, 1536, 1024, 384
+FLOPS = 2 * K * H * S + 2 * 2 * H * N * S
+
+F32 = mybir.dt.float32
+BF16 = mybir.dt.bfloat16
+I32 = mybir.dt.int32
+U32 = mybir.dt.uint32
+U16 = mybir.dt.uint16
+U8 = mybir.dt.uint8
+FP8X4 = mybir.dt.float8_e4m3fn_x4
+FP4X4 = mybir.dt.float4_e2m1fn_x4
+ACT = mybir.ActivationFunctionType
+ALU = mybir.AluOpType
+
+P = 128
+PACK = 4
+KP = P * PACK
+KA = K // KP
+HB = H // KP
+HALF = 512
+NH = S // HALF
+NT = N // P
+CAST_LAG = 2
+EVAC = "SSSSSSSS"
+PAGE = "VVVVSSSS"
+CAST = "SSSSSSSVS"
+PW = "VVVVVVVV"
+PROD = "FFFFFFFF"
+W1SHARE = [0,0,0]
+WEAVE0 = "VVV"
+W5 = "VS"
+W5_AT = [5,8]
+W1_AT = [0,1,2]
+X0_AT = [5,6]
+PIECES = 2
+HBUFS = 2
+
+
+def tile_list_fresco_crack_fill_kernel(
+    tc, tab_words, tab_scales, offs, pos1, pos2, w1, slope, thr, paint, skip, wgs, gain, w4_words, w4_scales, w5, out
+):
+    nc = tc.nc
+    with ExitStack() as ctx:
+        keep = ctx.enter_context(tc.tile_pool(name="keep", bufs=1))
+        work = ctx.enter_context(tc.tile_pool(name="work", bufs=2))
+        psum = ctx.enter_context(tc.psum_pool(name="psum", bufs=1))
+
+        offs_t = keep.tile([P, S // 16], U16, name="offs_t")
+        pos1_t = keep.tile([P, PICK // 16], U16, name="pos1_t")
+        pos2_t = keep.tile([P, PICK // 16], U16, name="pos2_t")
+
+        def big(i, shape, dtype, name):
+            return keep.tile(shape, dtype, name=name, tag="big%d" % i, align_bytes=64)
+
+        def small(i, shape, dtype, name):
+            return keep.tile(shape, dtype, name=name, tag="small%d" % i, align_bytes=64)
+
+        def bank(i, name):
+            return psum.tile([P, HALF], F32, name=name, tag="bank%d" % i)
+
+        def load_table(a):
+            words = big(a, [P, T], U32, "tab%d" % a)
+            nc.sync.dma_start(
+                out=words[:].bitcast(I32), in_=tab_words[a].rearrange("p t i -> p (t i)").bitcast(I32)
+            )
+            return words
+
+        def load_w1(raw, a, b):
+            rows = w1[KP * a : KP * (a + 1), KP * b : KP * (b + 1)]
+            nc.sync.dma_start(out=raw[:], in_=rows.rearrange("(p j) c -> p j c", j=PACK))
+            return raw
+
+        def load_vec(vec, name):
+            tile = keep.tile([P, HB * PACK], F32, name=name)
+            nc.sync.dma_start(
+                out=tile[:].rearrange("p (b t) -> p b t", t=PACK), in_=vec.rearrange("(b p t) -> p b t", p=P, t=PACK)
+            )
+            return tile
+
+        def load_paint(tile, b, t0, t1):
+            rows = paint[KP * b : KP * (b + 1), :].rearrange("(p t) m -> p t m", t=PACK)
+            nc.sync.dma_start(out=tile[:, t0:t1, :], in_=rows[:, t0:t1, :])
+
+        tab_sc = keep.tile([P, T], U8, name="tab_sc", align_bytes=64)
+        nc.gpsimd.memset(tab_sc[:].bitcast(I32), 0)
+        tab = [load_table(0)]
+        nc.sync.dma_start(offs_t[:], offs)
+        for q in range(4):
+            nc.sync.dma_start(
+                out=tab_sc[32 * q : 32 * q + 4 * KA, :].bitcast(I32),
+                in_=tab_scales[:, 4 * q : 4 * q + 4, :].bitcast(I32),
+            )
+        raw1 = {}
+        raw1[0, 0] = load_w1(small(0, [P, PACK, KP], F32, "raw00"), 0, 0)
+        tab.append(load_table(1))
+        nc.sync.dma_start(pos1_t[:], pos1)
+        raw1[1, 0] = load_w1(small(1, [P, PACK, KP], F32, "raw10"), 1, 0)
+        nc.sync.dma_start(pos2_t[:], pos2)
+        slope_t = load_vec(slope, "slope_t")
+        tab.append(load_table(2))
+        thr_t = load_vec(thr, "thr_t")
+        skip_t = load_vec(skip, "skip_t")
+        raw1[2, 0] = load_w1(small(2, [P, PACK, KP], F32, "raw20"), 2, 0)
+        wgs_t = keep.tile([P, PACK, PICK], F32, name="wgs_t")
+        for q in range(4):
+            nc.sync.dma_start(out=wgs_t[32 * q : 32 * q + 32], in_=wgs.rearrange("(p t) m -> p t m", t=PACK))
+        pw = [keep.tile([P, PACK, PICK], F32, name="pw0")]
+        load_paint(pw[0], 0, 0, 2)
+        gain_t = load_vec(gain, "gain_t")
+        load_paint(pw[0], 0, 2, 4)
+
+        v_words = [keep.tile([P, S], U32, name="v_words%d" % a, align_bytes=64) for a in range(KA)]
+        v_sc = keep.tile([P, S], U8, name="v_sc", align_bytes=64)
+        w1_words = {}
+        w1_sc = {}
+
+        def round_w1(a, b, share):
+            grouped = work.tile([P, KP * PACK], BF16, name="grouped", tag="grouped", bufs=3, align_bytes=64)
+            dst = grouped[:].rearrange("p (t m j) -> p m t j", t=PACK, j=PACK)
+            src = raw1[a, b][:].rearrange("p j (m t) -> p m t j", t=PACK)
+            if share > 0:
+                nc.vector.tensor_copy(out=dst[:, :share], in_=src[:, :share])
+            if share < P:
+                nc.scalar.copy(out=dst[:, share:], in_=src[:, share:])
+            return grouped
+
+        def quantise_w1(a, b, grouped):
+            w1_words[a, b] = keep.tile([P, KP], U32, name="w1_words%d%d" % (a, b), align_bytes=64)
+            w1_sc[a, b] = keep.tile([P, KP], U8, name="w1_sc%d%d" % (a, b), align_bytes=64)
+            nc.vector.quantize_mx(out=w1_words[a, b][:].bitcast(FP8X4), scales=w1_sc[a, b][:], in_=grouped[:])
+
+        for a in range(KA):
+            nc.vector.tensor_copy(v_words[a][:], tab[a][:].indirect(offs_t[:]))
+            if a == 0:
+                nc.vector.tensor_copy(v_sc[:], tab_sc[:].indirect(offs_t[:]))
+            quantise_w1(a, 0, round_w1(a, 0, 64 if a == KA - 1 else 0))
+
+        for a in range(KA):
+            raw1[a, 1] = load_w1(big(a, [P, PACK, KP], F32, "raw%d1" % a), a, 1)
+        pw.append(small(2, [P, PACK, PICK], F32, "pw1"))
+        load_paint(pw[1], 1, 0, 4)
+        w4_w = small(0, [P, HB, 2 * N], U8, "w4_w")
+        nc.sync.dma_start(out=w4_w[:].bitcast(I32), in_=w4_words.rearrange("b p c -> p b c").bitcast(I32))
+        w4_sc = small(1, [P, HB, N], U8, "w4_sc")
+        nc.gpsimd.memset(w4_sc[:].bitcast(I32), 0)
+        for q in range(4):
+            nc.sync.dma_start(
+                out=w4_sc[32 * q : 32 * q + 4].bitcast(I32),
+                in_=w4_scales[:, 4 * q : 4 * q + 4, :].rearrange("b r c -> r b c").bitcast(I32),
+            )
+
+        h_banks = {}
+
+        def h_pass(b, t, a):
+            for hf in range(NH):
+                if a == 0:
+                    h_banks[b, t, hf] = bank(NH * t + hf, "hb%d%d%d" % (b, t, hf))
+                cols = slice(HALF * hf, HALF * (hf + 1))
+                wc = slice(P * t, P * (t + 1))
+                nc.tensor.matmul_mx(
+                    out=h_banks[b, t, hf][:],
+                    lhsT=w1_words[a, b][:, wc].bitcast(FP8X4),
+                    lhsT_scale=w1_sc[a, b][:, wc],
+                    rhs=v_words[a][:, cols].bitcast(FP8X4),
+                    rhs_scale=v_sc[4 * a :, cols],
+                    start=(a == 0),
+                    stop=(a == KA - 1),
+                )
+
+        def scale_rows(eng, dst, src, col):
+            if eng == "S":
+                nc.scalar.activation(out=dst, in_=src, func=ACT.Copy, scale=col)
+            elif eng == "V":
+                nc.vector.tensor_scalar(dst, src, col, None, ALU.mult)
+            else:
+                nc.gpsimd.tensor_scalar(dst, src, col, 0.0, ALU.mult, ALU.add)
+
+        def move(eng, dst, src):
+            if eng == "S":
+                nc.scalar.copy(out=dst, in_=src)
+            else:
+                nc.vector.tensor_copy(out=dst, in_=src)
+
+        def product(eng, dst, x, y):
+            (nc.vector if eng == "V" else nc.gpsimd).tensor_tensor(dst, x, y, ALU.mult)
+
+        def weigh_paint(b, t):
+            product(PW[PACK * b + t], pw[b][:, t, :], pw[b][:, t, :], wgs_t[:, t, :])
+
+        pages = {}
+
+        def make_page(b, t):
+            k = PACK * b + t
+            h = work.tile([P, S], F32, name="h", tag="h", bufs=HBUFS)
+            page = work.tile([P, S], F32, name="page", tag="page", bufs=4)
+            look = work.tile([P, PICK], F32, name="look", tag="look", bufs=3)
+            for hf in range(NH):
+                move(EVAC[k], h[:, HALF * hf : HALF * (hf + 1)], h_banks[b, t, hf][:])
+            if PAGE[k] == "S":
+                for hf in range(NH):
+                    scale_rows("S", page[:, HALF * hf : HALF * (hf + 1)], h_banks[b, t, hf][:], skip_t[:, k : k + 1])
+            else:
+                scale_rows(PAGE[k], page[:], h[:], skip_t[:, k : k + 1])
+            nc.scalar.activation(
+                out=look[:], in_=h[:].indirect(pos1_t[:]), func=ACT.Sigmoid,
+                bias=thr_t[:, k : k + 1], scale=slope_t[:, k : k + 1],
+            )
+            if PROD[k] == "F":
+                nc.vector.tensor_tensor(page[:].indirect(pos2_t[:]), look[:], pw[b][:, t, :], ALU.mult)
+            else:
+                put = work.tile([P, PICK], F32, name="put", tag="put", bufs=3)
+                product(PROD[k], put[:], look[:], pw[b][:, t, :])
+                nc.vector.tensor_copy(page[:].indirect(pos2_t[:]), put[:])
+            pages[b, t] = page
+
+        planes = [work.tile([P, PACK, S], BF16, name="planes%d" % b, tag="planes") for b in range(HB)]
+        x_words = [keep.tile([P, S], U32, name="x_words%d" % b, align_bytes=64) for b in range(HB)]
+        x_sc = [keep.tile([P, S], U8, name="x_sc%d" % b, align_bytes=64) for b in range(HB)]
+
+        def round_x(b, t):
+            k = PACK * b + t
+            scale_rows(CAST[k], planes[b][:, t, :], pages[b, t][:], gain_t[:, k : k + 1])
+
+        def weave_x(eng, b, hf, pieces):
+            cols = slice(HALF * hf, HALF * (hf + 1))
+            grouped = work.tile([P, HALF * PACK], BF16, name="grouped", tag="grouped", bufs=3, align_bytes=64)
+            dst = grouped[:].rearrange("p (c i t) -> p c t i", i=4, t=PACK)
+            src = planes[b][:, :, cols].rearrange("p t (c i) -> p c t i", i=4)
+            for c0 in range(0, P, P // pieces):
+                move(eng, dst[:, c0 : c0 + P // pieces], src[:, c0 : c0 + P // pieces])
+            return grouped
+
+        def quantise_x(b, hf, grouped):
+            cols = slice(HALF * hf, HALF * (hf + 1))
+            nc.vector.quantize_mx(out=x_words[b][:, cols].bitcast(FP8X4), scales=x_sc[b][:, cols], in_=grouped[:])
+
+        w5_words = []
+        w5_sc = []
+
+        def prepare_w5(b):
+            raw = big(b, [P, PACK, N], F32, "raw5%d" % b)
+            nc.sync.dma_start(out=raw[:], in_=w5[KP * b : KP * (b + 1), :].rearrange("(p j) c -> p j c", j=PACK))
+            grouped = work.tile([P, N * PACK], BF16, name="grouped", tag="grouped", bufs=3, align_bytes=64)
+            move(
+                W5[b],
+                grouped[:].rearrange("p (c i j) -> p c j i", i=4, j=PACK),
+                raw[:].rearrange("p j (c i) -> p c j i", i=4),
+            )
+            w5_words.append(keep.tile([P, N], U32, name="w5_words%d" % b, align_bytes=64))
+            w5_sc.append(keep.tile([P, N], U8, name="w5_sc%d" % b, align_bytes=64))
+            nc.vector.quantize_mx(out=w5_words[b][:].bitcast(FP8X4), scales=w5_sc[b][:], in_=grouped[:])
+
+        for a in range(KA):
+            for t in range(PACK):
+                h_pass(0, t, a)
+
+        order = [(b, t) for b in range(HB) for t in range(PACK)]
+        last = len(order) - 1
+        for i, (b, t) in enumerate(order):
+            weigh_paint(b, t)
+            if b == 1:
+                for a in range(KA):
+                    h_pass(b, t, a)
+            make_page(b, t)
+            for a in range(KA):
+                if W1_AT[a] == i:
+                    quantise_w1(a, 1, round_w1(a, 1, W1SHARE[a]))
+            if i >= CAST_LAG:
+                round_x(*order[i - CAST_LAG])
+            for hf in range(NH):
+                if X0_AT[hf] == i:
+                    quantise_x(0, hf, weave_x(WEAVE0[hf], 0, hf, 1))
+            for b5 in range(HB):
+                if W5_AT[b5] == i:
+                    prepare_w5(b5)
+        for b, t in order[last + 1 - CAST_LAG : last]:
+            round_x(b, t)
+        for b5 in range(HB):
+            if W5_AT[b5] > last:
+                prepare_w5(b5)
+        for hf in range(NH):
+            cols = slice(HALF * hf, HALF * (hf + 1))
+            scale_rows(CAST[last + hf], planes[1][:, PACK - 1, cols], pages[order[last]][:, cols], gain_t[:, last : last + 1])
+        for hf in range(NH):
+            quantise_x(1, hf, weave_x(WEAVE0[2], 1, hf, PIECES))
+
+        units = [(hf, n) for hf in range(NH) for n in range(NT)]
+        for u, (hf, n) in enumerate(units):
+            cols = slice(HALF * hf, HALF * (hf + 1))
+            wc = slice(P * n, P * (n + 1))
+            wavy = bank((2 * u) % 8, "wavy%d" % u)
+            flat = bank((2 * u + 1) % 8, "flat%d" % u)
+            for b in range(HB):
+                nc.tensor.matmul_mx(
+                    out=wavy[:], lhsT=w5_words[b][:, wc].bitcast(FP8X4), lhsT_scale=w5_sc[b][:, wc],
+                    rhs=x_words[b][:, cols].bitcast(FP8X4), rhs_scale=x_sc[b][:, cols],
+                    start=(b == 0), stop=(b == HB - 1),
+                )
+            for b in range(HB):
+                nc.tensor.matmul_mx(
+                    out=flat[:], lhsT=w4_w[:, b, 2 * P * n : 2 * P * (n + 1)].bitcast(FP4X4),
+                    lhsT_scale=w4_sc[:, b, wc],
+                    rhs=x_words[b][:, cols].bitcast(FP8X4), rhs_scale=x_sc[b][:, cols],
+                    start=(b == 0), stop=(b == HB - 1),
+                )
+            third = work.tile([P, HALF], F32, name="third", tag="third", bufs=3)
+            square = work.tile([P, HALF], F32, name="square", tag="square")
+            cubic = work.tile([P, HALF], F32, name="cubic", tag="cubic")
+            result = work.tile([P, HALF], F32, name="result", tag="result", bufs=6)
+            nc.scalar.activation(out=third[:], in_=wavy[:], func=ACT.Sin, scale=1.0 / 3.0)
+            nc.scalar.activation(out=square[:], in_=third[:], func=ACT.Square)
+            nc.vector.scalar_tensor_tensor(cubic[:], square[:], 0.75, third[:], ALU.subtract, ALU.mult)
+            nc.vector.scalar_tensor_tensor(result[:], cubic[:], -4.0, flat[:], ALU.mult, ALU.add)
+            nc.sync.dma_start(out=out[wc, cols], in_=result[:])

@@ -1,6 +1,7 @@
 from contextlib import ExitStack
 
 import concourse.mybir as mybir
+from concourse.masks import make_identity
 
 T, S, PICK, K, H, N = 4096, 1024, 512, 1536, 1024, 384
 FLOPS = 2 * K * H * S + 2 * 2 * H * N * S
@@ -25,7 +26,7 @@ HALF = 512
 NH = S // HALF
 NT = N // P
 CAST_LAG = 2
-EVAC = "SSSSSSSS"
+EVAC = "XSSSSSSS"
 PAGE = "VVVVSSSS"
 CAST = "SSSSSSSVS"
 PW = "VVVVVVVV"
@@ -34,9 +35,12 @@ W1SHARE = [0,0,0]
 WEAVE0 = "VVV"
 W5 = "VS"
 W5_AT = [5,8]
-W1_AT = [0,1,2]
-X0_AT = [5,6]
+W1_AT = [1,2,2]
+X0_AT = [4,5]
 PIECES = 2
+LOADS = ["p01","p23","r0","r1","r2","p47","f0","w0","w1","s0"]
+CAST_AT = [3,3,4,4,6,8,8]
+LOOKBUFS = 2
 HBUFS = 2
 
 
@@ -85,33 +89,46 @@ def tile_list_fresco_crack_fill_kernel(
             rows = paint[KP * b : KP * (b + 1), :].rearrange("(p t) m -> p t m", t=PACK)
             nc.sync.dma_start(out=tile[:, t0:t1, :], in_=rows[:, t0:t1, :])
 
-        tab_sc = keep.tile([P, T], U8, name="tab_sc", align_bytes=64)
-        nc.gpsimd.memset(tab_sc[:].bitcast(I32), 0)
+        ident = keep.tile([P, P], F32, name="ident")
+        make_identity(nc, ident[:])
+        wgs_rows = keep.tile([P, PICK], F32, name="wgs_rows")
+        nc.sync.dma_start(out=wgs_rows[:], in_=wgs)
         tab = [load_table(0)]
         nc.sync.dma_start(offs_t[:], offs)
+        nc.sync.dma_start(pos1_t[:], pos1)
+        nc.sync.dma_start(pos2_t[:], pos2)
+        slope_t = load_vec(slope, "slope_t")
+        thr_t = load_vec(thr, "thr_t")
+        skip_t = load_vec(skip, "skip_t")
+        tab_sc = keep.tile([P, T], U8, name="tab_sc", align_bytes=64)
+        nc.gpsimd.memset(tab_sc[:].bitcast(I32), 0)
         for q in range(4):
-            nc.sync.dma_start(
+            nc.gpsimd.dma_start(
                 out=tab_sc[32 * q : 32 * q + 4 * KA, :].bitcast(I32),
                 in_=tab_scales[:, 4 * q : 4 * q + 4, :].bitcast(I32),
             )
         raw1 = {}
         raw1[0, 0] = load_w1(small(0, [P, PACK, KP], F32, "raw00"), 0, 0)
         tab.append(load_table(1))
-        nc.sync.dma_start(pos1_t[:], pos1)
-        raw1[1, 0] = load_w1(small(1, [P, PACK, KP], F32, "raw10"), 1, 0)
-        nc.sync.dma_start(pos2_t[:], pos2)
-        slope_t = load_vec(slope, "slope_t")
-        tab.append(load_table(2))
-        thr_t = load_vec(thr, "thr_t")
-        skip_t = load_vec(skip, "skip_t")
-        raw1[2, 0] = load_w1(small(2, [P, PACK, KP], F32, "raw20"), 2, 0)
-        wgs_t = keep.tile([P, PACK, PICK], F32, name="wgs_t")
-        for q in range(4):
-            nc.sync.dma_start(out=wgs_t[32 * q : 32 * q + 32], in_=wgs.rearrange("(p t) m -> p t m", t=PACK))
-        pw = [keep.tile([P, PACK, PICK], F32, name="pw0")]
-        load_paint(pw[0], 0, 0, 2)
         gain_t = load_vec(gain, "gain_t")
-        load_paint(pw[0], 0, 2, 4)
+        raw1[1, 0] = load_w1(small(1, [P, PACK, KP], F32, "raw10"), 1, 0)
+        raw1[2, 0] = load_w1(small(2, [P, PACK, KP], F32, "raw20"), 2, 0)
+        tab.append(load_table(2))
+
+        turned = bank(0, "turned")
+        for c in range(PICK // P):
+            nc.tensor.transpose(turned[:, P * c : P * (c + 1)], wgs_rows[:, P * c : P * (c + 1)], ident[:])
+        dealt = work.tile([P, PICK // P, PACK, P], F32, name="dealt", tag="planes", bufs=1)
+        nc.scalar.copy(
+            out=dealt[:].rearrange("m c t (g q) -> m c t g q", g=4),
+            in_=turned[:].rearrange("m (c q t) -> m c t q", t=PACK, q=32).unsqueeze(3).to_broadcast([P, PICK // P, PACK, 4, 32]),
+        )
+        wgs_t = keep.tile([P, PACK, PICK], F32, name="wgs_t")
+        for t in range(PACK):
+            back = bank(1 + t, "back%d" % t)
+            for c in range(PICK // P):
+                nc.tensor.transpose(back[:, P * c : P * (c + 1)], dealt[:, c, t, :], ident[:])
+            nc.scalar.copy(out=wgs_t[:, t, :], in_=back[:])
 
         v_words = [keep.tile([P, S], U32, name="v_words%d" % a, align_bytes=64) for a in range(KA)]
         v_sc = keep.tile([P, S], U8, name="v_sc", align_bytes=64)
@@ -134,24 +151,44 @@ def tile_list_fresco_crack_fill_kernel(
             nc.vector.quantize_mx(out=w1_words[a, b][:].bitcast(FP8X4), scales=w1_sc[a, b][:], in_=grouped[:])
 
         for a in range(KA):
-            nc.vector.tensor_copy(v_words[a][:], tab[a][:].indirect(offs_t[:]))
+            quantise_w1(a, 0, round_w1(a, 0, 0))
+            for hf in range(NH):
+                nc.vector.tensor_copy(
+                    v_words[a][:, HALF * hf : HALF * (hf + 1)],
+                    tab[a][:].indirect(offs_t[:, HALF // 16 * hf : HALF // 16 * (hf + 1)]),
+                )
             if a == 0:
                 nc.vector.tensor_copy(v_sc[:], tab_sc[:].indirect(offs_t[:]))
-            quantise_w1(a, 0, round_w1(a, 0, 64 if a == KA - 1 else 0))
 
-        for a in range(KA):
-            raw1[a, 1] = load_w1(big(a, [P, PACK, KP], F32, "raw%d1" % a), a, 1)
-        pw.append(small(2, [P, PACK, PICK], F32, "pw1"))
-        load_paint(pw[1], 1, 0, 4)
-        w4_w = small(0, [P, HB, 2 * N], U8, "w4_w")
-        nc.sync.dma_start(out=w4_w[:].bitcast(I32), in_=w4_words.rearrange("b p c -> p b c").bitcast(I32))
-        w4_sc = small(1, [P, HB, N], U8, "w4_sc")
+        paint_t = [keep.tile([P, PACK, PICK], F32, name="paint0"), small(2, [P, PACK, PICK], F32, "paint1")]
+        w4_w = keep.tile([P, HB, 2 * N], U8, name="w4_w", align_bytes=64)
+        w4_sc = keep.tile([P, HB, N], U8, name="w4_sc", align_bytes=64)
         nc.gpsimd.memset(w4_sc[:].bitcast(I32), 0)
-        for q in range(4):
-            nc.sync.dma_start(
-                out=w4_sc[32 * q : 32 * q + 4].bitcast(I32),
-                in_=w4_scales[:, 4 * q : 4 * q + 4, :].rearrange("b r c -> r b c").bitcast(I32),
-            )
+        raw5 = {}
+        for item in LOADS:
+            lo, hi = int(item[1]), int(item[-1]) + 1
+            if item[0] == "g":
+                for q in (0, 2, 1, 3):
+                    nc.sync.dma_start(
+                        out=wgs_t[32 * q : 32 * q + 32, lo:hi, :], in_=wgs.rearrange("(p t) m -> p t m", t=PACK)[:, lo:hi, :]
+                    )
+            elif item[0] == "p":
+                load_paint(paint_t[lo // PACK], lo // PACK, lo % PACK, (hi - 1) % PACK + 1)
+            elif item[0] == "r":
+                raw1[lo, 1] = load_w1(big(lo, [P, PACK, KP], F32, "raw%d1" % lo), lo, 1)
+            elif item[0] == "f":
+                nc.sync.dma_start(out=w4_w[:].bitcast(I32), in_=w4_words.rearrange("b p c -> p b c").bitcast(I32))
+            elif item[0] == "s":
+                for q in range(4):
+                    nc.gpsimd.dma_start(
+                        out=w4_sc[32 * q : 32 * q + 4].bitcast(I32),
+                        in_=w4_scales[:, 4 * q : 4 * q + 4, :].rearrange("b r c -> r b c").bitcast(I32),
+                    )
+            else:
+                raw5[lo] = small(lo, [P, PACK, N], F32, "raw5%d" % lo)
+                nc.sync.dma_start(
+                    out=raw5[lo][:], in_=w5[KP * lo : KP * (lo + 1), :].rearrange("(p j) c -> p j c", j=PACK)
+                )
 
         h_banks = {}
 
@@ -188,18 +225,21 @@ def tile_list_fresco_crack_fill_kernel(
         def product(eng, dst, x, y):
             (nc.vector if eng == "V" else nc.gpsimd).tensor_tensor(dst, x, y, ALU.mult)
 
+        pw = {}
+
         def weigh_paint(b, t):
-            product(PW[PACK * b + t], pw[b][:, t, :], pw[b][:, t, :], wgs_t[:, t, :])
+            pw[b, t] = work.tile([P, PICK], F32, name="pw", tag="pw", bufs=4)
+            product(PW[PACK * b + t], pw[b, t][:], paint_t[b][:, t, :], wgs_t[:, t, :])
 
         pages = {}
 
         def make_page(b, t):
             k = PACK * b + t
-            h = work.tile([P, S], F32, name="h", tag="h", bufs=HBUFS)
+            h = work.tile([P, S], F32, name="h", tag="h%d" % b, bufs=HBUFS if b == 0 else 2)
             page = work.tile([P, S], F32, name="page", tag="page", bufs=4)
-            look = work.tile([P, PICK], F32, name="look", tag="look", bufs=3)
+            look = work.tile([P, PICK], F32, name="look", tag="look%d" % b, bufs=LOOKBUFS if b == 0 else 2)
             for hf in range(NH):
-                move(EVAC[k], h[:, HALF * hf : HALF * (hf + 1)], h_banks[b, t, hf][:])
+                move("SV"[hf] if EVAC[k] == "X" else EVAC[k], h[:, HALF * hf : HALF * (hf + 1)], h_banks[b, t, hf][:])
             if PAGE[k] == "S":
                 for hf in range(NH):
                     scale_rows("S", page[:, HALF * hf : HALF * (hf + 1)], h_banks[b, t, hf][:], skip_t[:, k : k + 1])
@@ -210,14 +250,14 @@ def tile_list_fresco_crack_fill_kernel(
                 bias=thr_t[:, k : k + 1], scale=slope_t[:, k : k + 1],
             )
             if PROD[k] == "F":
-                nc.vector.tensor_tensor(page[:].indirect(pos2_t[:]), look[:], pw[b][:, t, :], ALU.mult)
+                nc.vector.tensor_tensor(page[:].indirect(pos2_t[:]), look[:], pw[b, t][:], ALU.mult)
             else:
                 put = work.tile([P, PICK], F32, name="put", tag="put", bufs=3)
-                product(PROD[k], put[:], look[:], pw[b][:, t, :])
+                product(PROD[k], put[:], look[:], pw[b, t][:])
                 nc.vector.tensor_copy(page[:].indirect(pos2_t[:]), put[:])
             pages[b, t] = page
 
-        planes = [work.tile([P, PACK, S], BF16, name="planes%d" % b, tag="planes") for b in range(HB)]
+        planes = [raw1[2, 1][:].bitcast(BF16), work.tile([P, PACK, S], BF16, name="planes1", tag="planes", bufs=1)]
         x_words = [keep.tile([P, S], U32, name="x_words%d" % b, align_bytes=64) for b in range(HB)]
         x_sc = [keep.tile([P, S], U8, name="x_sc%d" % b, align_bytes=64) for b in range(HB)]
 
@@ -242,8 +282,7 @@ def tile_list_fresco_crack_fill_kernel(
         w5_sc = []
 
         def prepare_w5(b):
-            raw = big(b, [P, PACK, N], F32, "raw5%d" % b)
-            nc.sync.dma_start(out=raw[:], in_=w5[KP * b : KP * (b + 1), :].rearrange("(p j) c -> p j c", j=PACK))
+            raw = raw5[b]
             grouped = work.tile([P, N * PACK], BF16, name="grouped", tag="grouped", bufs=3, align_bytes=64)
             move(
                 W5[b],
@@ -269,16 +308,18 @@ def tile_list_fresco_crack_fill_kernel(
             for a in range(KA):
                 if W1_AT[a] == i:
                     quantise_w1(a, 1, round_w1(a, 1, W1SHARE[a]))
-            if i >= CAST_LAG:
-                round_x(*order[i - CAST_LAG])
+            for j in range(last):
+                if CAST_AT[j] == i:
+                    round_x(*order[j])
             for hf in range(NH):
                 if X0_AT[hf] == i:
                     quantise_x(0, hf, weave_x(WEAVE0[hf], 0, hf, 1))
             for b5 in range(HB):
                 if W5_AT[b5] == i:
                     prepare_w5(b5)
-        for b, t in order[last + 1 - CAST_LAG : last]:
-            round_x(b, t)
+        for j in range(last):
+            if CAST_AT[j] > last:
+                round_x(*order[j])
         for b5 in range(HB):
             if W5_AT[b5] > last:
                 prepare_w5(b5)
@@ -310,7 +351,7 @@ def tile_list_fresco_crack_fill_kernel(
             third = work.tile([P, HALF], F32, name="third", tag="third", bufs=3)
             square = work.tile([P, HALF], F32, name="square", tag="square")
             cubic = work.tile([P, HALF], F32, name="cubic", tag="cubic")
-            result = work.tile([P, HALF], F32, name="result", tag="result", bufs=6)
+            result = work.tile([P, HALF], F32, name="result", tag="result", bufs=4)
             nc.scalar.activation(out=third[:], in_=wavy[:], func=ACT.Sin, scale=1.0 / 3.0)
             nc.scalar.activation(out=square[:], in_=third[:], func=ACT.Square)
             nc.vector.scalar_tensor_tensor(cubic[:], square[:], 0.75, third[:], ALU.subtract, ALU.mult)

@@ -1,3 +1,4 @@
+import math
 from contextlib import ExitStack
 
 import concourse.mybir as mybir
@@ -19,29 +20,16 @@ ALU = mybir.AluOpType
 
 P = 128
 PACK = 4
-KP = P * PACK
-KA = K // KP
-HB = H // KP
-HALF = 512
-NH = S // HALF
-NT = N // P
-CAST_LAG = 2
-EVAC = "XSSSSSSS"
-PAGE = "VVVVSSSS"
-CAST = "SSSSSSSVS"
-PW = "VVVVVVVV"
-PROD = "FFFFFFFF"
-W1SHARE = [0,0,0]
-WEAVE0 = "VVV"
-W5 = "VS"
-W5_AT = [5,8]
-W1_AT = [1,2,2]
-X0_AT = [4,5]
-PIECES = 2
-LOADS = ["p01","p23","r0","r1","r2","p47","f0","w0","w1","s0"]
-CAST_AT = [3,3,4,4,6,8,8]
-LOOKBUFS = 2
-HBUFS = 2
+PASS = P * PACK
+K_PASSES = K // PASS
+GROUPS = H // PASS
+BANK = 512
+BANKS = 8
+HALVES = S // BANK
+QUADRANTS = 4
+QUAD = P // QUADRANTS
+LIST_ROWS = 16
+RUN = 4
 
 
 def tile_list_fresco_crack_fill_kernel(
@@ -53,307 +41,288 @@ def tile_list_fresco_crack_fill_kernel(
         work = ctx.enter_context(tc.tile_pool(name="work", bufs=2))
         psum = ctx.enter_context(tc.psum_pool(name="psum", bufs=1))
 
-        offs_t = keep.tile([P, S // 16], U16, name="offs_t")
-        pos1_t = keep.tile([P, PICK // 16], U16, name="pos1_t")
-        pos2_t = keep.tile([P, PICK // 16], U16, name="pos2_t")
+        offs_t = keep.tile([P, S // LIST_ROWS], U16, name="offs_t")
+        pos1_t = keep.tile([P, PICK // LIST_ROWS], U16, name="pos1_t")
+        pos2_t = keep.tile([P, PICK // LIST_ROWS], U16, name="pos2_t")
 
-        def big(i, shape, dtype, name):
-            return keep.tile(shape, dtype, name=name, tag="big%d" % i, align_bytes=64)
+        def table_slot(a, shape, dtype, name):
+            return keep.tile(shape, dtype, name=name, tag="table_slot%d" % a, align_bytes=64)
 
-        def small(i, shape, dtype, name):
-            return keep.tile(shape, dtype, name=name, tag="small%d" % i, align_bytes=64)
+        def w1_slot(a, shape, name):
+            return keep.tile(shape, F32, name=name, tag="w1_slot%d" % a, align_bytes=64)
 
-        def bank(i, name):
-            return psum.tile([P, HALF], F32, name=name, tag="bank%d" % i)
+        def bank(index, name):
+            return psum.tile([P, BANK], F32, name=name, tag="bank%d" % index)
+
+        def half(hf):
+            return slice(BANK * hf, BANK * (hf + 1))
+
+        def woven_tile(width):
+            return work.tile([P, width * PACK], BF16, name="woven", tag="woven", bufs=3, align_bytes=64)
 
         def load_table(a):
-            words = big(a, [P, T], U32, "tab%d" % a)
-            nc.sync.dma_start(
-                out=words[:].bitcast(I32), in_=tab_words[a].rearrange("p t i -> p (t i)").bitcast(I32)
-            )
+            words = table_slot(a, [P, T], U32, "tab%d" % a)
+            nc.sync.dma_start(out=words[:].bitcast(I32), in_=tab_words[a].rearrange("p t i -> p (t i)").bitcast(I32))
             return words
 
-        def load_w1(raw, a, b):
-            rows = w1[KP * a : KP * (a + 1), KP * b : KP * (b + 1)]
-            nc.sync.dma_start(out=raw[:], in_=rows.rearrange("(p j) c -> p j c", j=PACK))
-            return raw
+        def load_by_four(tile, rows):
+            nc.sync.dma_start(out=tile, in_=rows.rearrange("(p j) c -> p j c", j=PACK))
 
-        def load_vec(vec, name):
-            tile = keep.tile([P, HB * PACK], F32, name=name)
+        def load_w1(tile, a, g):
+            load_by_four(tile[:], w1[PASS * a : PASS * (a + 1), PASS * g : PASS * (g + 1)])
+            return tile
+
+        def load_row_values(values, name):
+            tile = keep.tile([P, GROUPS * PACK], F32, name=name)
             nc.sync.dma_start(
-                out=tile[:].rearrange("p (b t) -> p b t", t=PACK), in_=vec.rearrange("(b p t) -> p b t", p=P, t=PACK)
+                out=tile[:].rearrange("p (g i) -> p g i", i=PACK), in_=values.rearrange("(g p i) -> p g i", p=P, i=PACK)
             )
             return tile
 
-        def load_paint(tile, b, t0, t1):
-            rows = paint[KP * b : KP * (b + 1), :].rearrange("(p t) m -> p t m", t=PACK)
-            nc.sync.dma_start(out=tile[:, t0:t1, :], in_=rows[:, t0:t1, :])
+        tab_sc = keep.tile([P, T], U8, name="tab_sc", align_bytes=64)
+        nc.vector.memset(tab_sc[:].bitcast(I32), 0)
+        for q in range(QUADRANTS):
+            nc.gpsimd.dma_start(
+                out=tab_sc[QUAD * q : QUAD * q + 4 * K_PASSES, :].bitcast(I32),
+                in_=tab_scales[:, 4 * q : 4 * q + 4, :].bitcast(I32),
+            )
+        one = keep.tile([P, 1], F32, name="one")
+        nc.vector.memset(one[:], 1.0)
+        shift = keep.tile([P, 1], F32, name="shift")
+        nc.vector.tensor_scalar(shift[:], one[:], -math.pi / 4, None, ALU.mult)
 
-        ident = keep.tile([P, P], F32, name="ident")
-        make_identity(nc, ident[:])
         wgs_rows = keep.tile([P, PICK], F32, name="wgs_rows")
         nc.sync.dma_start(out=wgs_rows[:], in_=wgs)
         tab = [load_table(0)]
         nc.sync.dma_start(offs_t[:], offs)
         nc.sync.dma_start(pos1_t[:], pos1)
         nc.sync.dma_start(pos2_t[:], pos2)
-        slope_t = load_vec(slope, "slope_t")
-        thr_t = load_vec(thr, "thr_t")
-        skip_t = load_vec(skip, "skip_t")
-        tab_sc = keep.tile([P, T], U8, name="tab_sc", align_bytes=64)
-        nc.gpsimd.memset(tab_sc[:].bitcast(I32), 0)
-        for q in range(4):
-            nc.gpsimd.dma_start(
-                out=tab_sc[32 * q : 32 * q + 4 * KA, :].bitcast(I32),
-                in_=tab_scales[:, 4 * q : 4 * q + 4, :].bitcast(I32),
-            )
-        raw1 = {}
-        raw1[0, 0] = load_w1(small(0, [P, PACK, KP], F32, "raw00"), 0, 0)
+        slope_t = load_row_values(slope, "slope_t")
+        thr_t = load_row_values(thr, "thr_t")
+        skip_t = load_row_values(skip, "skip_t")
+        w1_raw = {}
+        w1_raw[0, 0] = load_w1(w1_slot(0, [P, PACK, PASS], "w1_raw00"), 0, 0)
         tab.append(load_table(1))
-        gain_t = load_vec(gain, "gain_t")
-        raw1[1, 0] = load_w1(small(1, [P, PACK, KP], F32, "raw10"), 1, 0)
-        raw1[2, 0] = load_w1(small(2, [P, PACK, KP], F32, "raw20"), 2, 0)
+        gain_t = load_row_values(gain, "gain_t")
+        for a in range(1, K_PASSES):
+            w1_raw[a, 0] = load_w1(w1_slot(a, [P, PACK, PASS], "w1_raw%d0" % a), a, 0)
         tab.append(load_table(2))
 
+        ident = keep.tile([P, P], F32, name="ident")
+        make_identity(nc, ident[:])
+        chunks = PICK // P
         turned = bank(0, "turned")
-        for c in range(PICK // P):
+        for c in range(chunks):
             nc.tensor.transpose(turned[:, P * c : P * (c + 1)], wgs_rows[:, P * c : P * (c + 1)], ident[:])
-        dealt = work.tile([P, PICK // P, PACK, P], F32, name="dealt", tag="planes", bufs=1)
+        dealt = work.tile([P, chunks, PACK, P], F32, name="dealt", tag="rounded", bufs=1)
         nc.scalar.copy(
-            out=dealt[:].rearrange("m c t (g q) -> m c t g q", g=4),
-            in_=turned[:].rearrange("m (c q t) -> m c t q", t=PACK, q=32).unsqueeze(3).to_broadcast([P, PICK // P, PACK, 4, 32]),
+            out=dealt[:].rearrange("m c i (q s) -> m c i q s", q=QUADRANTS),
+            in_=turned[:]
+            .rearrange("m (c s i) -> m c i s", i=PACK, s=QUAD)
+            .unsqueeze(3)
+            .to_broadcast([P, chunks, PACK, QUADRANTS, QUAD]),
         )
         wgs_t = keep.tile([P, PACK, PICK], F32, name="wgs_t")
-        for t in range(PACK):
-            back = bank(1 + t, "back%d" % t)
-            for c in range(PICK // P):
-                nc.tensor.transpose(back[:, P * c : P * (c + 1)], dealt[:, c, t, :], ident[:])
-            nc.scalar.copy(out=wgs_t[:, t, :], in_=back[:])
+        for i in range(PACK):
+            back = bank(1 + i, "back%d" % i)
+            for c in range(chunks):
+                nc.tensor.transpose(back[:, P * c : P * (c + 1)], dealt[:, c, i, :], ident[:])
+            nc.scalar.copy(out=wgs_t[:, i, :], in_=back[:])
 
-        v_words = [keep.tile([P, S], U32, name="v_words%d" % a, align_bytes=64) for a in range(KA)]
+        v_words = [keep.tile([P, S], U32, name="v_words%d" % a, align_bytes=64) for a in range(K_PASSES)]
         v_sc = keep.tile([P, S], U8, name="v_sc", align_bytes=64)
         w1_words = {}
         w1_sc = {}
 
-        def round_w1(a, b, share):
-            grouped = work.tile([P, KP * PACK], BF16, name="grouped", tag="grouped", bufs=3, align_bytes=64)
-            dst = grouped[:].rearrange("p (t m j) -> p m t j", t=PACK, j=PACK)
-            src = raw1[a, b][:].rearrange("p j (m t) -> p m t j", t=PACK)
-            if share > 0:
-                nc.vector.tensor_copy(out=dst[:, :share], in_=src[:, :share])
-            if share < P:
-                nc.scalar.copy(out=dst[:, share:], in_=src[:, share:])
-            return grouped
+        def quantise_w1(a, g):
+            woven = woven_tile(PASS)
+            nc.scalar.copy(
+                out=woven[:].rearrange("p (i m j) -> p m i j", i=PACK, j=PACK),
+                in_=w1_raw[a, g][:].rearrange("p j (m i) -> p m i j", i=PACK),
+            )
+            w1_words[a, g] = keep.tile([P, PASS], U32, name="w1_words%d%d" % (a, g), align_bytes=64)
+            w1_sc[a, g] = keep.tile([P, PASS], U8, name="w1_sc%d%d" % (a, g), align_bytes=64)
+            nc.vector.quantize_mx(out=w1_words[a, g][:].bitcast(FP8X4), scales=w1_sc[a, g][:], in_=woven[:])
 
-        def quantise_w1(a, b, grouped):
-            w1_words[a, b] = keep.tile([P, KP], U32, name="w1_words%d%d" % (a, b), align_bytes=64)
-            w1_sc[a, b] = keep.tile([P, KP], U8, name="w1_sc%d%d" % (a, b), align_bytes=64)
-            nc.vector.quantize_mx(out=w1_words[a, b][:].bitcast(FP8X4), scales=w1_sc[a, b][:], in_=grouped[:])
-
-        for a in range(KA):
-            quantise_w1(a, 0, round_w1(a, 0, 0))
-            for hf in range(NH):
-                nc.vector.tensor_copy(
-                    v_words[a][:, HALF * hf : HALF * (hf + 1)],
-                    tab[a][:].indirect(offs_t[:, HALF // 16 * hf : HALF // 16 * (hf + 1)]),
-                )
+        per_half = BANK // LIST_ROWS
+        for a in range(K_PASSES):
+            quantise_w1(a, 0)
+            for hf in range(HALVES):
+                entries = offs_t[:, per_half * hf : per_half * (hf + 1)]
+                nc.vector.tensor_copy(v_words[a][:, half(hf)], tab[a][:].indirect(entries))
             if a == 0:
                 nc.vector.tensor_copy(v_sc[:], tab_sc[:].indirect(offs_t[:]))
 
-        paint_t = [keep.tile([P, PACK, PICK], F32, name="paint0"), small(2, [P, PACK, PICK], F32, "paint1")]
-        w4_w = keep.tile([P, HB, 2 * N], U8, name="w4_w", align_bytes=64)
-        w4_sc = keep.tile([P, HB, N], U8, name="w4_sc", align_bytes=64)
-        nc.gpsimd.memset(w4_sc[:].bitcast(I32), 0)
-        raw5 = {}
-        for item in LOADS:
-            lo, hi = int(item[1]), int(item[-1]) + 1
-            if item[0] == "g":
-                for q in (0, 2, 1, 3):
-                    nc.sync.dma_start(
-                        out=wgs_t[32 * q : 32 * q + 32, lo:hi, :], in_=wgs.rearrange("(p t) m -> p t m", t=PACK)[:, lo:hi, :]
-                    )
-            elif item[0] == "p":
-                load_paint(paint_t[lo // PACK], lo // PACK, lo % PACK, (hi - 1) % PACK + 1)
-            elif item[0] == "r":
-                raw1[lo, 1] = load_w1(big(lo, [P, PACK, KP], F32, "raw%d1" % lo), lo, 1)
-            elif item[0] == "f":
-                nc.sync.dma_start(out=w4_w[:].bitcast(I32), in_=w4_words.rearrange("b p c -> p b c").bitcast(I32))
-            elif item[0] == "s":
-                for q in range(4):
-                    nc.gpsimd.dma_start(
-                        out=w4_sc[32 * q : 32 * q + 4].bitcast(I32),
-                        in_=w4_scales[:, 4 * q : 4 * q + 4, :].rearrange("b r c -> r b c").bitcast(I32),
-                    )
-            else:
-                raw5[lo] = small(lo, [P, PACK, N], F32, "raw5%d" % lo)
-                nc.sync.dma_start(
-                    out=raw5[lo][:], in_=w5[KP * lo : KP * (lo + 1), :].rearrange("(p j) c -> p j c", j=PACK)
-                )
+        paint_t = [keep.tile([P, PACK, PICK], F32, name="paint0"), w1_slot(2, [P, PACK, PICK], "paint1")]
+        w4_w = keep.tile([P, GROUPS, 2 * N], U8, name="w4_w", align_bytes=64)
+        w4_sc = keep.tile([P, GROUPS, N], U8, name="w4_sc", align_bytes=64)
+        nc.vector.memset(w4_sc[:].bitcast(I32), 0)
+        first_paint = paint[0:PASS, :].rearrange("(p i) m -> p i m", i=PACK)
+        for i in range(0, PACK, 2):
+            nc.sync.dma_start(out=paint_t[0][:, i : i + 2, :], in_=first_paint[:, i : i + 2, :])
+        for a in range(K_PASSES):
+            w1_raw[a, 1] = load_w1(table_slot(a, [P, PACK, PASS], F32, "w1_raw%d1" % a), a, 1)
+        load_by_four(paint_t[1][:], paint[PASS:H, :])
+        nc.sync.dma_start(out=w4_w[:].bitcast(I32), in_=w4_words.rearrange("g p c -> p g c").bitcast(I32))
+        w5_raw = []
+        for g in range(GROUPS):
+            w5_raw.append(w1_slot(g, [P, PACK, N], "w5_raw%d" % g))
+            load_by_four(w5_raw[g][:], w5[PASS * g : PASS * (g + 1), :])
+        for q in range(QUADRANTS):
+            nc.sync.dma_start(
+                out=w4_sc[QUAD * q : QUAD * q + 4].bitcast(I32),
+                in_=w4_scales[:, 4 * q : 4 * q + 4, :].rearrange("g r c -> r g c").bitcast(I32),
+            )
 
         h_banks = {}
 
-        def h_pass(b, t, a):
-            for hf in range(NH):
+        def h_pass(g, i, a):
+            rows = slice(P * i, P * (i + 1))
+            for hf in range(HALVES):
                 if a == 0:
-                    h_banks[b, t, hf] = bank(NH * t + hf, "hb%d%d%d" % (b, t, hf))
-                cols = slice(HALF * hf, HALF * (hf + 1))
-                wc = slice(P * t, P * (t + 1))
+                    h_banks[g, i, hf] = bank(HALVES * i + hf, "h_bank%d%d%d" % (g, i, hf))
                 nc.tensor.matmul_mx(
-                    out=h_banks[b, t, hf][:],
-                    lhsT=w1_words[a, b][:, wc].bitcast(FP8X4),
-                    lhsT_scale=w1_sc[a, b][:, wc],
-                    rhs=v_words[a][:, cols].bitcast(FP8X4),
-                    rhs_scale=v_sc[4 * a :, cols],
+                    out=h_banks[g, i, hf][:],
+                    lhsT=w1_words[a, g][:, rows].bitcast(FP8X4),
+                    lhsT_scale=w1_sc[a, g][:, rows],
+                    rhs=v_words[a][:, half(hf)].bitcast(FP8X4),
+                    rhs_scale=v_sc[4 * a :, half(hf)],
                     start=(a == 0),
-                    stop=(a == KA - 1),
+                    stop=(a == K_PASSES - 1),
                 )
 
-        def scale_rows(eng, dst, src, col):
-            if eng == "S":
-                nc.scalar.activation(out=dst, in_=src, func=ACT.Copy, scale=col)
-            elif eng == "V":
-                nc.vector.tensor_scalar(dst, src, col, None, ALU.mult)
-            else:
-                nc.gpsimd.tensor_scalar(dst, src, col, 0.0, ALU.mult, ALU.add)
+        weight = {}
 
-        def move(eng, dst, src):
-            if eng == "S":
-                nc.scalar.copy(out=dst, in_=src)
-            else:
-                nc.vector.tensor_copy(out=dst, in_=src)
-
-        def product(eng, dst, x, y):
-            (nc.vector if eng == "V" else nc.gpsimd).tensor_tensor(dst, x, y, ALU.mult)
-
-        pw = {}
-
-        def weigh_paint(b, t):
-            pw[b, t] = work.tile([P, PICK], F32, name="pw", tag="pw", bufs=4)
-            product(PW[PACK * b + t], pw[b, t][:], paint_t[b][:, t, :], wgs_t[:, t, :])
+        def weigh_paint(g, i):
+            weight[g, i] = work.tile([P, PICK], F32, name="weight", tag="weight", bufs=PACK)
+            nc.vector.tensor_tensor(weight[g, i][:], paint_t[g][:, i, :], wgs_t[:, i, :], ALU.mult)
 
         pages = {}
 
-        def make_page(b, t):
-            k = PACK * b + t
-            h = work.tile([P, S], F32, name="h", tag="h%d" % b, bufs=HBUFS if b == 0 else 2)
-            page = work.tile([P, S], F32, name="page", tag="page", bufs=4)
-            look = work.tile([P, PICK], F32, name="look", tag="look%d" % b, bufs=LOOKBUFS if b == 0 else 2)
-            for hf in range(NH):
-                move("SV"[hf] if EVAC[k] == "X" else EVAC[k], h[:, HALF * hf : HALF * (hf + 1)], h_banks[b, t, hf][:])
-            if PAGE[k] == "S":
-                for hf in range(NH):
-                    scale_rows("S", page[:, HALF * hf : HALF * (hf + 1)], h_banks[b, t, hf][:], skip_t[:, k : k + 1])
+        def make_page(g, i):
+            col = slice(PACK * g + i, PACK * g + i + 1)
+            h = work.tile([P, S], F32, name="h", tag="h%d" % g)
+            page = work.tile([P, S], F32, name="page", tag="page", bufs=PACK + 1)
+            look = work.tile([P, PICK], F32, name="look", tag="look%d" % g)
+            nc.scalar.copy(out=h[:, half(0)], in_=h_banks[g, i, 0][:])
+            if (g, i) == (0, 0):
+                nc.vector.tensor_copy(out=h[:, half(1)], in_=h_banks[g, i, 1][:])
             else:
-                scale_rows(PAGE[k], page[:], h[:], skip_t[:, k : k + 1])
+                nc.scalar.copy(out=h[:, half(1)], in_=h_banks[g, i, 1][:])
+            if g == 0:
+                nc.vector.tensor_scalar(page[:], h[:], skip_t[:, col], None, ALU.mult)
+            else:
+                for hf in range(HALVES):
+                    nc.scalar.activation(
+                        out=page[:, half(hf)], in_=h_banks[g, i, hf][:], func=ACT.Copy, scale=skip_t[:, col]
+                    )
             nc.scalar.activation(
-                out=look[:], in_=h[:].indirect(pos1_t[:]), func=ACT.Sigmoid,
-                bias=thr_t[:, k : k + 1], scale=slope_t[:, k : k + 1],
+                out=look[:], in_=h[:].indirect(pos1_t[:]), func=ACT.Sigmoid, bias=thr_t[:, col], scale=slope_t[:, col]
             )
-            if PROD[k] == "F":
-                nc.vector.tensor_tensor(page[:].indirect(pos2_t[:]), look[:], pw[b, t][:], ALU.mult)
-            else:
-                put = work.tile([P, PICK], F32, name="put", tag="put", bufs=3)
-                product(PROD[k], put[:], look[:], pw[b, t][:])
-                nc.vector.tensor_copy(page[:].indirect(pos2_t[:]), put[:])
-            pages[b, t] = page
+            nc.vector.tensor_tensor(page[:].indirect(pos2_t[:]), look[:], weight[g, i][:], ALU.mult)
+            pages[g, i] = page
 
-        planes = [raw1[2, 1][:].bitcast(BF16), work.tile([P, PACK, S], BF16, name="planes1", tag="planes", bufs=1)]
-        x_words = [keep.tile([P, S], U32, name="x_words%d" % b, align_bytes=64) for b in range(HB)]
-        x_sc = [keep.tile([P, S], U8, name="x_sc%d" % b, align_bytes=64) for b in range(HB)]
+        rounded = [
+            w1_raw[K_PASSES - 1, 1][:].bitcast(BF16),
+            work.tile([P, PACK, S], BF16, name="rounded1", tag="rounded", bufs=1),
+        ]
+        x_words = [keep.tile([P, S], U32, name="x_words%d" % g, align_bytes=64) for g in range(GROUPS)]
+        x_sc = [keep.tile([P, S], U8, name="x_sc%d" % g, align_bytes=64) for g in range(GROUPS)]
 
-        def round_x(b, t):
-            k = PACK * b + t
-            scale_rows(CAST[k], planes[b][:, t, :], pages[b, t][:], gain_t[:, k : k + 1])
+        def round_page(g, i, cols):
+            col = slice(PACK * g + i, PACK * g + i + 1)
+            nc.scalar.activation(
+                out=rounded[g][:, i, cols], in_=pages[g, i][:, cols], func=ACT.Copy, scale=gain_t[:, col]
+            )
 
-        def weave_x(eng, b, hf, pieces):
-            cols = slice(HALF * hf, HALF * (hf + 1))
-            grouped = work.tile([P, HALF * PACK], BF16, name="grouped", tag="grouped", bufs=3, align_bytes=64)
-            dst = grouped[:].rearrange("p (c i t) -> p c t i", i=4, t=PACK)
-            src = planes[b][:, :, cols].rearrange("p t (c i) -> p c t i", i=4)
-            for c0 in range(0, P, P // pieces):
-                move(eng, dst[:, c0 : c0 + P // pieces], src[:, c0 : c0 + P // pieces])
-            return grouped
-
-        def quantise_x(b, hf, grouped):
-            cols = slice(HALF * hf, HALF * (hf + 1))
-            nc.vector.quantize_mx(out=x_words[b][:, cols].bitcast(FP8X4), scales=x_sc[b][:, cols], in_=grouped[:])
+        def quantise_x(g, hf):
+            woven = woven_tile(BANK)
+            nc.vector.tensor_copy(
+                out=woven[:].rearrange("p (c e i) -> p c i e", e=RUN, i=PACK),
+                in_=rounded[g][:, :, half(hf)].rearrange("p i (c e) -> p c i e", e=RUN),
+            )
+            nc.vector.quantize_mx(
+                out=x_words[g][:, half(hf)].bitcast(FP8X4), scales=x_sc[g][:, half(hf)], in_=woven[:]
+            )
 
         w5_words = []
         w5_sc = []
 
-        def prepare_w5(b):
-            raw = raw5[b]
-            grouped = work.tile([P, N * PACK], BF16, name="grouped", tag="grouped", bufs=3, align_bytes=64)
-            move(
-                W5[b],
-                grouped[:].rearrange("p (c i j) -> p c j i", i=4, j=PACK),
-                raw[:].rearrange("p j (c i) -> p c j i", i=4),
+        def quantise_w5(g, copy):
+            woven = woven_tile(N)
+            copy(
+                out=woven[:].rearrange("p (c e j) -> p c j e", e=RUN, j=PACK),
+                in_=w5_raw[g][:].rearrange("p j (c e) -> p c j e", e=RUN),
             )
-            w5_words.append(keep.tile([P, N], U32, name="w5_words%d" % b, align_bytes=64))
-            w5_sc.append(keep.tile([P, N], U8, name="w5_sc%d" % b, align_bytes=64))
-            nc.vector.quantize_mx(out=w5_words[b][:].bitcast(FP8X4), scales=w5_sc[b][:], in_=grouped[:])
+            w5_words.append(keep.tile([P, N], U32, name="w5_words%d" % g, align_bytes=64))
+            w5_sc.append(keep.tile([P, N], U8, name="w5_sc%d" % g, align_bytes=64))
+            nc.vector.quantize_mx(out=w5_words[g][:].bitcast(FP8X4), scales=w5_sc[g][:], in_=woven[:])
 
-        for a in range(KA):
-            for t in range(PACK):
-                h_pass(0, t, a)
+        whole = slice(0, S)
 
-        order = [(b, t) for b in range(HB) for t in range(PACK)]
-        last = len(order) - 1
-        for i, (b, t) in enumerate(order):
-            weigh_paint(b, t)
-            if b == 1:
-                for a in range(KA):
-                    h_pass(b, t, a)
-            make_page(b, t)
-            for a in range(KA):
-                if W1_AT[a] == i:
-                    quantise_w1(a, 1, round_w1(a, 1, W1SHARE[a]))
-            for j in range(last):
-                if CAST_AT[j] == i:
-                    round_x(*order[j])
-            for hf in range(NH):
-                if X0_AT[hf] == i:
-                    quantise_x(0, hf, weave_x(WEAVE0[hf], 0, hf, 1))
-            for b5 in range(HB):
-                if W5_AT[b5] == i:
-                    prepare_w5(b5)
-        for j in range(last):
-            if CAST_AT[j] > last:
-                round_x(*order[j])
-        for b5 in range(HB):
-            if W5_AT[b5] > last:
-                prepare_w5(b5)
-        for hf in range(NH):
-            cols = slice(HALF * hf, HALF * (hf + 1))
-            scale_rows(CAST[last + hf], planes[1][:, PACK - 1, cols], pages[order[last]][:, cols], gain_t[:, last : last + 1])
-        for hf in range(NH):
-            quantise_x(1, hf, weave_x(WEAVE0[2], 1, hf, PIECES))
+        for a in range(K_PASSES):
+            for i in range(PACK):
+                h_pass(0, i, a)
+        for i in range(PACK):
+            weigh_paint(0, i)
+            make_page(0, i)
+            if i == PACK - 2:
+                for a in range(K_PASSES):
+                    quantise_w1(a, 1)
 
-        units = [(hf, n) for hf in range(NH) for n in range(NT)]
-        for u, (hf, n) in enumerate(units):
-            cols = slice(HALF * hf, HALF * (hf + 1))
-            wc = slice(P * n, P * (n + 1))
-            wavy = bank((2 * u) % 8, "wavy%d" % u)
-            flat = bank((2 * u + 1) % 8, "flat%d" % u)
-            for b in range(HB):
+        for i in range(PACK):
+            weigh_paint(1, i)
+            for a in range(K_PASSES):
+                h_pass(1, i, a)
+            make_page(1, i)
+            if i == 0:
+                for done in range(PACK):
+                    round_page(0, done, whole)
+                for hf in range(HALVES):
+                    quantise_x(0, hf)
+        for i in range(PACK - 1):
+            round_page(1, i, whole)
+        quantise_w5(0, nc.vector.tensor_copy)
+        quantise_w5(1, nc.scalar.copy)
+        nc.vector.tensor_scalar(
+            rounded[1][:, PACK - 1, half(0)], pages[1, PACK - 1][:, half(0)], gain_t[:, PACK * GROUPS - 1 :], None, ALU.mult
+        )
+        round_page(1, PACK - 1, half(1))
+        for hf in range(HALVES):
+            quantise_x(1, hf)
+
+        parts = [(hf, n) for hf in range(HALVES) for n in range(N // P)]
+        for u, (hf, n) in enumerate(parts):
+            rows = slice(P * n, P * (n + 1))
+            wavy = bank((2 * u) % BANKS, "wavy%d" % u)
+            flat = bank((2 * u + 1) % BANKS, "flat%d" % u)
+            for g in range(GROUPS):
                 nc.tensor.matmul_mx(
-                    out=wavy[:], lhsT=w5_words[b][:, wc].bitcast(FP8X4), lhsT_scale=w5_sc[b][:, wc],
-                    rhs=x_words[b][:, cols].bitcast(FP8X4), rhs_scale=x_sc[b][:, cols],
-                    start=(b == 0), stop=(b == HB - 1),
+                    out=wavy[:],
+                    lhsT=w5_words[g][:, rows].bitcast(FP8X4),
+                    lhsT_scale=w5_sc[g][:, rows],
+                    rhs=x_words[g][:, half(hf)].bitcast(FP8X4),
+                    rhs_scale=x_sc[g][:, half(hf)],
+                    start=(g == 0),
+                    stop=(g == GROUPS - 1),
                 )
-            for b in range(HB):
+            for g in range(GROUPS):
                 nc.tensor.matmul_mx(
-                    out=flat[:], lhsT=w4_w[:, b, 2 * P * n : 2 * P * (n + 1)].bitcast(FP4X4),
-                    lhsT_scale=w4_sc[:, b, wc],
-                    rhs=x_words[b][:, cols].bitcast(FP8X4), rhs_scale=x_sc[b][:, cols],
-                    start=(b == 0), stop=(b == HB - 1),
+                    out=flat[:],
+                    lhsT=w4_w[:, g, 2 * P * n : 2 * P * (n + 1)].bitcast(FP4X4),
+                    lhsT_scale=w4_sc[:, g, rows],
+                    rhs=x_words[g][:, half(hf)].bitcast(FP8X4),
+                    rhs_scale=x_sc[g][:, half(hf)],
+                    start=(g == 0),
+                    stop=(g == GROUPS - 1),
                 )
-            third = work.tile([P, HALF], F32, name="third", tag="third", bufs=3)
-            square = work.tile([P, HALF], F32, name="square", tag="square")
-            cubic = work.tile([P, HALF], F32, name="cubic", tag="cubic")
-            result = work.tile([P, HALF], F32, name="result", tag="result", bufs=4)
-            nc.scalar.activation(out=third[:], in_=wavy[:], func=ACT.Sin, scale=1.0 / 3.0)
-            nc.scalar.activation(out=square[:], in_=third[:], func=ACT.Square)
-            nc.vector.scalar_tensor_tensor(cubic[:], square[:], 0.75, third[:], ALU.subtract, ALU.mult)
-            nc.vector.scalar_tensor_tensor(result[:], cubic[:], -4.0, flat[:], ALU.mult, ALU.add)
-            nc.sync.dma_start(out=out[wc, cols], in_=result[:])
+            sine = work.tile([P, BANK], F32, name="sine", tag="sine", bufs=N // P)
+            twice_sq = work.tile([P, BANK], F32, name="twice_sq", tag="twice_sq")
+            result = work.tile([P, BANK], F32, name="result", tag="result", bufs=len(parts))
+            nc.scalar.activation(out=sine[:], in_=wavy[:], func=ACT.Sin, scale=0.5, bias=shift[:])
+            if hf == 0:
+                nc.vector.scalar_tensor_tensor(twice_sq[:], sine[:], 2.0, sine[:], ALU.mult, ALU.mult)
+            else:
+                nc.scalar.activation(out=twice_sq[:], in_=sine[:], func=ACT.Square, scale=math.sqrt(2.0))
+            nc.vector.scalar_tensor_tensor(result[:], flat[:], 1.0, twice_sq[:], ALU.add, ALU.subtract)
+            nc.sync.dma_start(out=out[rows, half(hf)], in_=result[:])

@@ -235,12 +235,15 @@ def tile_list_fresco_crack_fill_kernel(
                 out=rounded[g][:, i, cols], in_=pages[g, i][:, cols], func=ACT.Copy, scale=gain_t[:, col]
             )
 
-        def quantise_x(g, hf):
+        def weave_x(g, hf):
             woven = woven_tile(BANK)
             nc.vector.tensor_copy(
                 out=woven[:].rearrange("p (c e i) -> p c i e", e=RUN, i=PACK),
                 in_=rounded[g][:, :, half(hf)].rearrange("p i (c e) -> p c i e", e=RUN),
             )
+            return woven
+
+        def quantise_x(g, hf, woven):
             nc.vector.quantize_mx(
                 out=x_words[g][:, half(hf)].bitcast(FP8X4), scales=x_sc[g][:, half(hf)], in_=woven[:]
             )
@@ -248,9 +251,9 @@ def tile_list_fresco_crack_fill_kernel(
         w5_words = []
         w5_sc = []
 
-        def quantise_w5(g, copy):
+        def quantise_w5(g):
             woven = woven_tile(N)
-            copy(
+            nc.scalar.copy(
                 out=woven[:].rearrange("p (c e j) -> p c j e", e=RUN, j=PACK),
                 in_=w5_raw[g][:].rearrange("p j (c e) -> p c j e", e=RUN),
             )
@@ -266,9 +269,10 @@ def tile_list_fresco_crack_fill_kernel(
         for i in range(PACK):
             weigh_paint(0, i)
             make_page(0, i)
-            if i == PACK - 2:
-                for a in range(K_PASSES):
-                    quantise_w1(a, 1)
+            if i < K_PASSES:
+                quantise_w1(i, 1)
+
+        quantise_w5(0)
 
         for i in range(PACK):
             weigh_paint(1, i)
@@ -278,21 +282,25 @@ def tile_list_fresco_crack_fill_kernel(
             if i == 0:
                 for done in range(PACK):
                     round_page(0, done, whole)
+                first_x = [weave_x(0, hf) for hf in range(HALVES)]
                 for hf in range(HALVES):
-                    quantise_x(0, hf)
+                    quantise_x(0, hf, first_x[hf])
         for i in range(PACK - 1):
             round_page(1, i, whole)
-        quantise_w5(0, nc.vector.tensor_copy)
-        quantise_w5(1, nc.scalar.copy)
-        nc.vector.tensor_scalar(
-            rounded[1][:, PACK - 1, half(0)], pages[1, PACK - 1][:, half(0)], gain_t[:, PACK * GROUPS - 1 :], None, ALU.mult
-        )
-        round_page(1, PACK - 1, half(1))
+        quantise_w5(1)
+        last = PACK - 1
+        last_gain = gain_t[:, PACK * GROUPS - 1 :]
+        nc.vector.tensor_scalar(rounded[1][:, last, half(0)], pages[1, last][:, half(0)], last_gain, None, ALU.mult)
+        round_page(1, last, half(1))
         for hf in range(HALVES):
-            quantise_x(1, hf)
+            quantise_x(1, hf, weave_x(1, hf))
 
         parts = [(hf, n) for hf in range(HALVES) for n in range(N // P)]
-        for u, (hf, n) in enumerate(parts):
+        flats, sines, squares = {}, {}, {}
+        stages = 3
+
+        def take_sine(u):
+            hf, n = parts[u]
             rows = slice(P * n, P * (n + 1))
             wavy = bank((2 * u) % BANKS, "wavy%d" % u)
             flat = bank((2 * u + 1) % BANKS, "flat%d" % u)
@@ -316,13 +324,24 @@ def tile_list_fresco_crack_fill_kernel(
                     start=(g == 0),
                     stop=(g == GROUPS - 1),
                 )
-            sine = work.tile([P, BANK], F32, name="sine", tag="sine", bufs=N // P)
-            twice_sq = work.tile([P, BANK], F32, name="twice_sq", tag="twice_sq")
-            result = work.tile([P, BANK], F32, name="result", tag="result", bufs=len(parts))
-            nc.scalar.activation(out=sine[:], in_=wavy[:], func=ACT.Sin, scale=0.5, bias=shift[:])
-            if hf == 0:
-                nc.vector.scalar_tensor_tensor(twice_sq[:], sine[:], 2.0, sine[:], ALU.mult, ALU.mult)
+            flats[u] = flat
+            sines[u] = work.tile([P, BANK], F32, name="sine", tag="sine", bufs=stages)
+            nc.scalar.activation(out=sines[u][:], in_=wavy[:], func=ACT.Sin, scale=0.5, bias=shift[:])
+
+        def square(u):
+            squares[u] = work.tile([P, BANK], F32, name="twice_sq", tag="twice_sq", bufs=stages)
+            if parts[u][0] == 0:
+                nc.vector.scalar_tensor_tensor(squares[u][:], sines[u][:], 2.0, sines[u][:], ALU.mult, ALU.mult)
             else:
-                nc.scalar.activation(out=twice_sq[:], in_=sine[:], func=ACT.Square, scale=math.sqrt(2.0))
-            nc.vector.scalar_tensor_tensor(result[:], flat[:], 1.0, twice_sq[:], ALU.add, ALU.subtract)
-            nc.sync.dma_start(out=out[rows, half(hf)], in_=result[:])
+                nc.scalar.activation(out=squares[u][:], in_=sines[u][:], func=ACT.Square, scale=math.sqrt(2.0))
+
+        def finish(u):
+            hf, n = parts[u]
+            result = work.tile([P, BANK], F32, name="result", tag="result", bufs=len(parts))
+            nc.vector.scalar_tensor_tensor(result[:], flats[u][:], 1.0, squares[u][:], ALU.add, ALU.subtract)
+            nc.sync.dma_start(out=out[P * n : P * (n + 1), half(hf)], in_=result[:])
+
+        for step in range(len(parts) + stages - 1):
+            for lag, stage in enumerate((take_sine, square, finish)):
+                if 0 <= step - lag < len(parts):
+                    stage(step - lag)

@@ -91,6 +91,9 @@ def tile_list_fresco_crack_fill_kernel(
         shift = keep.tile([P, 1], F32, name="shift")
         nc.vector.tensor_scalar(shift[:], one[:], -math.pi / 4, None, ALU.mult)
 
+        warm = keep.tile([P, 1], F32, name="warm")
+        nc.scalar.activation(out=warm[:], in_=one[:], func=ACT.Sigmoid)
+
         wgs_rows = keep.tile([P, PICK], F32, name="wgs_rows")
         nc.sync.dma_start(out=wgs_rows[:], in_=wgs)
         tab = [load_table(0)]

import math
from contextlib import ExitStack

import concourse.mybir as mybir
from concourse.masks import make_identity

T, S, PICK, K, H, N = 4096, 1024, 512, 1536, 1024, 384
FLOPS = 2 * K * H * S + 2 * 2 * H * N * S

F32 = mybir.dt.float32
BF16 = mybir.dt.bfloat16
I32 = mybir.dt.int32
U32 = mybir.dt.uint32
U16 = mybir.dt.uint16
U8 = mybir.dt.uint8
FP8X4 = mybir.dt.float8_e4m3fn_x4
FP4X4 = mybir.dt.float4_e2m1fn_x4
ACT = mybir.ActivationFunctionType
ALU = mybir.AluOpType

P = 128
PACK = 4
PASS = P * PACK
K_PASSES = K // PASS
GROUPS = H // PASS
BANK = 512
BANKS = 8
HALVES = S // BANK
QUADRANTS = 4
QUAD = P // QUADRANTS
LIST_ROWS = 16
RUN = 4


def tile_list_fresco_crack_fill_kernel(
    tc, tab_words, tab_scales, offs, pos1, pos2, w1, slope, thr, paint, skip, wgs, gain, w4_words, w4_scales, w5, out
):
    nc = tc.nc
    with ExitStack() as ctx:
        keep = ctx.enter_context(tc.tile_pool(name="keep", bufs=1))
        work = ctx.enter_context(tc.tile_pool(name="work", bufs=2))
        psum = ctx.enter_context(tc.psum_pool(name="psum", bufs=1))

        offs_t = keep.tile([P, S // LIST_ROWS], U16, name="offs_t")
        pos1_t = keep.tile([P, PICK // LIST_ROWS], U16, name="pos1_t")
        pos2_t = keep.tile([P, PICK // LIST_ROWS], U16, name="pos2_t")

        def table_slot(a, shape, dtype, name):
            return keep.tile(shape, dtype, name=name, tag="table_slot%d" % a, align_bytes=64)

        def w1_slot(a, shape, name):
            return keep.tile(shape, F32, name=name, tag="w1_slot%d" % a, align_bytes=64)

        def bank(index, name):
            return psum.tile([P, BANK], F32, name=name, tag="bank%d" % index)

        def half(hf):
            return slice(BANK * hf, BANK * (hf + 1))

        def woven_tile(width):
            return work.tile([P, width * PACK], BF16, name="woven", tag="woven", bufs=3, align_bytes=64)

        def load_table(a):
            words = table_slot(a, [P, T], U32, "tab%d" % a)
            nc.sync.dma_start(out=words[:].bitcast(I32), in_=tab_words[a].rearrange("p t i -> p (t i)").bitcast(I32))
            return words

        def load_by_four(tile, rows):
            nc.sync.dma_start(out=tile, in_=rows.rearrange("(p j) c -> p j c", j=PACK))

        def load_w1(tile, a, g):
            load_by_four(tile[:], w1[PASS * a : PASS * (a + 1), PASS * g : PASS * (g + 1)])
            return tile

        def load_row_values(values, name):
            tile = keep.tile([P, GROUPS * PACK], F32, name=name)
            nc.sync.dma_start(
                out=tile[:].rearrange("p (g i) -> p g i", i=PACK), in_=values.rearrange("(g p i) -> p g i", p=P, i=PACK)
            )
            return tile

        tab_sc = keep.tile([P, T], U8, name="tab_sc", align_bytes=64)
        nc.vector.memset(tab_sc[:].bitcast(I32), 0)
        for q in range(QUADRANTS):
            nc.gpsimd.dma_start(
                out=tab_sc[QUAD * q : QUAD * q + 4 * K_PASSES, :].bitcast(I32),
                in_=tab_scales[:, 4 * q : 4 * q + 4, :].bitcast(I32),
            )
        one = keep.tile([P, 1], F32, name="one")
        nc.vector.memset(one[:], 1.0)
        shift = keep.tile([P, 1], F32, name="shift")
        nc.vector.tensor_scalar(shift[:], one[:], -math.pi / 4, None, ALU.mult)

        warm = keep.tile([P, 1], F32, name="warm")
        nc.scalar.activation(out=warm[:], in_=one[:], func=ACT.Sigmoid)

        wgs_rows = keep.tile([P, PICK], F32, name="wgs_rows")
        nc.sync.dma_start(out=wgs_rows[:], in_=wgs)
        tab = [load_table(0)]
        nc.sync.dma_start(offs_t[:], offs)
        nc.sync.dma_start(pos1_t[:], pos1)
        nc.sync.dma_start(pos2_t[:], pos2)
        slope_t = load_row_values(slope, "slope_t")
        thr_t = load_row_values(thr, "thr_t")
        skip_t = load_row_values(skip, "skip_t")
        w1_raw = {}
        w1_raw[0, 0] = load_w1(w1_slot(0, [P, PACK, PASS], "w1_raw00"), 0, 0)
        tab.append(load_table(1))
        gain_t = load_row_values(gain, "gain_t")
        for a in range(1, K_PASSES):
            w1_raw[a, 0] = load_w1(w1_slot(a, [P, PACK, PASS], "w1_raw%d0" % a), a, 0)
        tab.append(load_table(2))

        ident = keep.tile([P, P], F32, name="ident")
        make_identity(nc, ident[:])
        chunks = PICK // P
        turned = bank(0, "turned")
        for c in range(chunks):
            nc.tensor.transpose(turned[:, P * c : P * (c + 1)], wgs_rows[:, P * c : P * (c + 1)], ident[:])
        dealt = work.tile([P, chunks, PACK, P], F32, name="dealt", tag="rounded", bufs=1)
        nc.scalar.copy(
            out=dealt[:].rearrange("m c i (q s) -> m c i q s", q=QUADRANTS),
            in_=turned[:]
            .rearrange("m (c s i) -> m c i s", i=PACK, s=QUAD)
            .unsqueeze(3)
            .to_broadcast([P, chunks, PACK, QUADRANTS, QUAD]),
        )
        wgs_t = keep.tile([P, PACK, PICK], F32, name="wgs_t")
        for i in range(PACK):
            back = bank(1 + i, "back%d" % i)
            for c in range(chunks):
                nc.tensor.transpose(back[:, P * c : P * (c + 1)], dealt[:, c, i, :], ident[:])
            nc.scalar.copy(out=wgs_t[:, i, :], in_=back[:])

        v_words = [keep.tile([P, S], U32, name="v_words%d" % a, align_bytes=64) for a in range(K_PASSES)]
        v_sc = keep.tile([P, S], U8, name="v_sc", align_bytes=64)
        w1_words = {}
        w1_sc = {}

        def quantise_w1(a, g):
            woven = woven_tile(PASS)
            nc.scalar.copy(
                out=woven[:].rearrange("p (i m j) -> p m i j", i=PACK, j=PACK),
                in_=w1_raw[a, g][:].rearrange("p j (m i) -> p m i j", i=PACK),
            )
            w1_words[a, g] = keep.tile([P, PASS], U32, name="w1_words%d%d" % (a, g), align_bytes=64)
            w1_sc[a, g] = keep.tile([P, PASS], U8, name="w1_sc%d%d" % (a, g), align_bytes=64)
            nc.vector.quantize_mx(out=w1_words[a, g][:].bitcast(FP8X4), scales=w1_sc[a, g][:], in_=woven[:])

        per_half = BANK // LIST_ROWS
        for a in range(K_PASSES):
            quantise_w1(a, 0)
            for hf in range(HALVES):
                entries = offs_t[:, per_half * hf : per_half * (hf + 1)]
                nc.vector.tensor_copy(v_words[a][:, half(hf)], tab[a][:].indirect(entries))
            if a == 0:
                nc.vector.tensor_copy(v_sc[:], tab_sc[:].indirect(offs_t[:]))

        paint_t = [keep.tile([P, PACK, PICK], F32, name="paint0"), w1_slot(2, [P, PACK, PICK], "paint1")]
        w4_w = keep.tile([P, GROUPS, 2 * N], U8, name="w4_w", align_bytes=64)
        w4_sc = keep.tile([P, GROUPS, N], U8, name="w4_sc", align_bytes=64)
        nc.vector.memset(w4_sc[:].bitcast(I32), 0)
        first_paint = paint[0:PASS, :].rearrange("(p i) m -> p i m", i=PACK)
        for i in range(0, PACK, 2):
            nc.sync.dma_start(out=paint_t[0][:, i : i + 2, :], in_=first_paint[:, i : i + 2, :])
        for a in range(K_PASSES):
            w1_raw[a, 1] = load_w1(table_slot(a, [P, PACK, PASS], F32, "w1_raw%d1" % a), a, 1)
        load_by_four(paint_t[1][:], paint[PASS:H, :])
        nc.sync.dma_start(out=w4_w[:].bitcast(I32), in_=w4_words.rearrange("g p c -> p g c").bitcast(I32))
        w5_raw = []
        for g in range(GROUPS):
            w5_raw.append(w1_slot(g, [P, PACK, N], "w5_raw%d" % g))
            load_by_four(w5_raw[g][:], w5[PASS * g : PASS * (g + 1), :])
        for q in range(QUADRANTS):
            nc.sync.dma_start(
                out=w4_sc[QUAD * q : QUAD * q + 4].bitcast(I32),
                in_=w4_scales[:, 4 * q : 4 * q + 4, :].rearrange("g r c -> r g c").bitcast(I32),
            )

        h_banks = {}

        def h_pass(g, i, a):
            rows = slice(P * i, P * (i + 1))
            for hf in range(HALVES):
                if a == 0:
                    h_banks[g, i, hf] = bank(HALVES * i + hf, "h_bank%d%d%d" % (g, i, hf))
                nc.tensor.matmul_mx(
                    out=h_banks[g, i, hf][:],
                    lhsT=w1_words[a, g][:, rows].bitcast(FP8X4),
                    lhsT_scale=w1_sc[a, g][:, rows],
                    rhs=v_words[a][:, half(hf)].bitcast(FP8X4),
                    rhs_scale=v_sc[4 * a :, half(hf)],
                    start=(a == 0),
                    stop=(a == K_PASSES - 1),
                )

        weight = {}

        def weigh_paint(g, i):
            weight[g, i] = work.tile([P, PICK], F32, name="weight", tag="weight", bufs=PACK)
            nc.vector.tensor_tensor(weight[g, i][:], paint_t[g][:, i, :], wgs_t[:, i, :], ALU.mult)

        pages = {}

        def make_page(g, i):
            col = slice(PACK * g + i, PACK * g + i + 1)
            h = work.tile([P, S], F32, name="h", tag="h%d" % g)
            page = work.tile([P, S], F32, name="page", tag="page", bufs=PACK + 1)
            look = work.tile([P, PICK], F32, name="look", tag="look%d" % g)
            nc.scalar.copy(out=h[:, half(0)], in_=h_banks[g, i, 0][:])
            if (g, i) == (0, 0):
                nc.vector.tensor_copy(out=h[:, half(1)], in_=h_banks[g, i, 1][:])
            else:
                nc.scalar.copy(out=h[:, half(1)], in_=h_banks[g, i, 1][:])
            if g == 0:
                nc.vector.tensor_scalar(page[:], h[:], skip_t[:, col], None, ALU.mult)
            else:
                for hf in range(HALVES):
                    nc.scalar.activation(
                        out=page[:, half(hf)], in_=h_banks[g, i, hf][:], func=ACT.Copy, scale=skip_t[:, col]
                    )
            nc.scalar.activation(
                out=look[:], in_=h[:].indirect(pos1_t[:]), func=ACT.Sigmoid, bias=thr_t[:, col], scale=slope_t[:, col]
            )
            nc.vector.tensor_tensor(page[:].indirect(pos2_t[:]), look[:], weight[g, i][:], ALU.mult)
            pages[g, i] = page

        rounded = [
            w1_raw[K_PASSES - 1, 1][:].bitcast(BF16),
            work.tile([P, PACK, S], BF16, name="rounded1", tag="rounded", bufs=1),
        ]
        x_words = [keep.tile([P, S], U32, name="x_words%d" % g, align_bytes=64) for g in range(GROUPS)]
        x_sc = [keep.tile([P, S], U8, name="x_sc%d" % g, align_bytes=64) for g in range(GROUPS)]

        def round_page(g, i, cols):
            col = slice(PACK * g + i, PACK * g + i + 1)
            nc.scalar.activation(
                out=rounded[g][:, i, cols], in_=pages[g, i][:, cols], func=ACT.Copy, scale=gain_t[:, col]
            )

        def weave_x(g, hf):
            woven = woven_tile(BANK)
            nc.vector.tensor_copy(
                out=woven[:].rearrange("p (c e i) -> p c i e", e=RUN, i=PACK),
                in_=rounded[g][:, :, half(hf)].rearrange("p i (c e) -> p c i e", e=RUN),
            )
            return woven

        def quantise_x(g, hf, woven):
            nc.vector.quantize_mx(
                out=x_words[g][:, half(hf)].bitcast(FP8X4), scales=x_sc[g][:, half(hf)], in_=woven[:]
            )

        w5_words = []
        w5_sc = []

        def quantise_w5(g):
            woven = woven_tile(N)
            nc.scalar.copy(
                out=woven[:].rearrange("p (c e j) -> p c j e", e=RUN, j=PACK),
                in_=w5_raw[g][:].rearrange("p j (c e) -> p c j e", e=RUN),
            )
            w5_words.append(keep.tile([P, N], U32, name="w5_words%d" % g, align_bytes=64))
            w5_sc.append(keep.tile([P, N], U8, name="w5_sc%d" % g, align_bytes=64))
            nc.vector.quantize_mx(out=w5_words[g][:].bitcast(FP8X4), scales=w5_sc[g][:], in_=woven[:])

        whole = slice(0, S)

        for a in range(K_PASSES):
            for i in range(PACK):
                h_pass(0, i, a)
        for i in range(PACK):
            weigh_paint(0, i)
            make_page(0, i)
            if i < K_PASSES:
                quantise_w1(i, 1)

        quantise_w5(0)

        for i in range(PACK):
            weigh_paint(1, i)
            for a in range(K_PASSES):
                h_pass(1, i, a)
            make_page(1, i)
            if i == 0:
                for done in range(PACK):
                    round_page(0, done, whole)
                first_x = [weave_x(0, hf) for hf in range(HALVES)]
                for hf in range(HALVES):
                    quantise_x(0, hf, first_x[hf])
        for i in range(PACK - 1):
            round_page(1, i, whole)
        quantise_w5(1)
        last = PACK - 1
        last_gain = gain_t[:, PACK * GROUPS - 1 :]
        nc.vector.tensor_scalar(rounded[1][:, last, half(0)], pages[1, last][:, half(0)], last_gain, None, ALU.mult)
        round_page(1, last, half(1))
        for hf in range(HALVES):
            quantise_x(1, hf, weave_x(1, hf))

        parts = [(hf, n) for hf in range(HALVES) for n in range(N // P)]
        flats, sines, squares = {}, {}, {}
        stages = 3

        def take_sine(u):
            hf, n = parts[u]
            rows = slice(P * n, P * (n + 1))
            wavy = bank((2 * u) % BANKS, "wavy%d" % u)
            flat = bank((2 * u + 1) % BANKS, "flat%d" % u)
            for g in range(GROUPS):
                nc.tensor.matmul_mx(
                    out=wavy[:],
                    lhsT=w5_words[g][:, rows].bitcast(FP8X4),
                    lhsT_scale=w5_sc[g][:, rows],
                    rhs=x_words[g][:, half(hf)].bitcast(FP8X4),
                    rhs_scale=x_sc[g][:, half(hf)],
                    start=(g == 0),
                    stop=(g == GROUPS - 1),
                )
            for g in range(GROUPS):
                nc.tensor.matmul_mx(
                    out=flat[:],
                    lhsT=w4_w[:, g, 2 * P * n : 2 * P * (n + 1)].bitcast(FP4X4),
                    lhsT_scale=w4_sc[:, g, rows],
                    rhs=x_words[g][:, half(hf)].bitcast(FP8X4),
                    rhs_scale=x_sc[g][:, half(hf)],
                    start=(g == 0),
                    stop=(g == GROUPS - 1),
                )
            flats[u] = flat
            sines[u] = work.tile([P, BANK], F32, name="sine", tag="sine", bufs=stages)
            nc.scalar.activation(out=sines[u][:], in_=wavy[:], func=ACT.Sin, scale=0.5, bias=shift[:])

        def square(u):
            squares[u] = work.tile([P, BANK], F32, name="twice_sq", tag="twice_sq", bufs=stages)
            if parts[u][0] == 0:
                nc.vector.scalar_tensor_tensor(squares[u][:], sines[u][:], 2.0, sines[u][:], ALU.mult, ALU.mult)
            else:
                nc.scalar.activation(out=squares[u][:], in_=sines[u][:], func=ACT.Square, scale=math.sqrt(2.0))

        def finish(u):
            hf, n = parts[u]
            result = work.tile([P, BANK], F32, name="result", tag="result", bufs=len(parts))
            nc.vector.scalar_tensor_tensor(result[:], flats[u][:], 1.0, squares[u][:], ALU.add, ALU.subtract)
            nc.sync.dma_start(out=out[P * n : P * (n + 1), half(hf)], in_=result[:])

        for step in range(len(parts) + stages - 1):
            for lag, stage in enumerate((take_sine, square, finish)):
                if 0 <= step - lag < len(parts):
                    stage(step - lag)
